import numpy as np, ml_dtypes
CORES = [3,11,19,27,35,43,51,59]
N = 8
BF = ml_dtypes.bfloat16
def gentries(a):
    return np.ascontiguousarray(a.reshape(8, 16, -1).transpose(0, 2, 1)).reshape(8, -1)
def gtable(e):
    e = np.asarray(e); return np.ascontiguousarray(e.reshape(8, -1, 16).transpose(0, 2, 1)).reshape(128, -1).astype(np.int32)
NV, NT, NL, RO = 2048, 3072, 128, 4
def graphs(rng):
    tp = np.zeros((N, 8, 16, NT), np.int64); oc = np.zeros((N, 8, 16, NV), np.int64); c = 16 * NT // NV
    for n in range(N):
        for g in range(8):
            e = rng.permutation(16 * NT) % NV
            o = rng.permuted(np.argsort(e.astype(np.uint16), kind="stable").reshape(NV, c), axis=1)
            tp[n, g] = e.reshape(NT, 16).T; oc[n, g] = (o[:, np.arange(16) % c] // 16).T
    return tp, oc
def levels(rng, n):
    return np.floor(rng.random((N, 8, 16, n)) * rng.integers(65, 257, (N, 8, 1, n))).astype(np.int64)
def pack(dom, val, tp, oc, q):
    return {"dom": dom.reshape(N, 128, NV).astype(np.float32).astype(BF), "val": val.reshape(N, 128, NT).astype(np.float32).astype(BF),
            "tp": np.ascontiguousarray(tp.reshape(N, 128, NT)).astype(np.int32), "oc": np.ascontiguousarray(oc.reshape(N, 128, NV)).astype(np.int32), "q": np.stack([gtable(a) for a in q])}
def setup_inputs(rng):
    tp, oc = graphs(rng)
    return pack(levels(rng, NV), levels(rng, NT), tp, oc, rng.integers(0, NT, (N, 8, NL)))
def rolled(rng, n):
    base = rng.integers(0, 250, (N, 8, 16)); sh = rng.integers(0, 16, (N, 8, 1, n))
    x = np.take_along_axis(base, ((np.arange(16)[:, None] + sh) % 16).reshape(N, 8, 16 * n), 2).reshape(N, 8, 16, n)
    x[:, :, 3] += rng.random((N, 8, n)) < 0.1
    return x
def setup_inputs_ties(rng):
    tp, oc = graphs(rng)
    return pack(rolled(rng, NV), rolled(rng, NT), tp, oc, rng.integers(0, NT, (N, 8, NL)))
def setup_inputs_alike(rng):
    tp, oc = graphs(rng); dom = levels(rng, NV); val = levels(rng, NT); q = rng.integers(0, NT, (N, 8, NL))
    q[:, 0] = rng.integers(0, NT, (N, 1)); q[:, 1] = rng.choice(np.array([0, 5, NT - 1, NT - 2, NT // 2]), (N, NL)); q[:, 5] = rng.choice(np.array([0, NT - 1]), (N, NL))
    tp[:, 2] = tp[:, 2, :1]; oc[:, 3] = rng.choice(np.array([0, NT - 1]), (N, 16, NV)); tp[:, 4] = rng.choice(np.array([0, NV - 1, NV // 2]), (N, 16, NT))
    dom[:, 6, :, 7] = 255; np.put_along_axis(tp[:, 6], rng.integers(0, 16, (N, 1, NT)), 7, 1)
    q[:, 7] = 16 * np.argsort(rng.random((N, NT // 16)), axis=1)[:, np.arange(NL) % (NT // 16)] + rng.integers(0, 16, (N, 1))
    tp[:, 7] = 16 * (np.arange(NT) // 16 % (NV // 16)) + rng.integers(0, 16, (N, 1, 1))
    return pack(dom, val, tp, oc, q)
def setup_inputs_full(rng):
    p = np.argsort(rng.random((3, N, 8, NL)), axis=-1); cv = np.arange(NV); ct = np.arange(NT); dom = levels(rng, NV); val = levels(rng, NT)
    bt = rng.integers(0, NV // NL, (N, 8, 16, NT)); bo = rng.integers(0, NT // NL, (N, 8, 16, NV)); bq = rng.integers(0, NT // NL, (N, 8, NL))
    bt[:, 0] = 2 * rng.integers(0, NV // NL // 2, (N, 16, NT)) + (np.arange(N) % 2)[:, None, None]
    bt[:, 1] = rng.integers(0, NV // NL); bq[:, 1] = rng.integers(0, NT // NL); val[:, 1] //= 2
    lt = NT // NL // (RO + 1); lv = NV // NL // RO
    bq[:, 4] = rng.integers(0, lt, (N, NL))
    bt[:, 4] = lv * np.minimum(ct // NL // lt, RO - 1) + rng.integers(0, lv, (N, 16, NT))
    bo[:, 4] = lt * (np.minimum(cv // NL // lv, RO - 1) + 1) + rng.integers(0, lt, (N, 16, NV))
    tp = NL * bt + p[0][:, :, ct % NL][:, :, None, :]
    oc = NL * bo + p[1][:, :, cv % NL][:, :, None, :]
    q = NL * bq + p[2]
    tab = NL * rng.integers(0, NV // NL, (N, 16, NL // 2)) + np.arange(NL // 2)
    tp[:, 2] = np.take_along_axis(tab, (p[0][:, 2][:, ct % NL] // 2)[:, None, :], 2)
    k = (rng.integers(0, NL, (N, 1, NV)) + (NL // 16) * np.arange(16)[:, None]) % NL
    oc[:, 3] = np.take_along_axis(np.repeat(q[:, 3][:, None, :], 16, axis=1), k, 2)
    return pack(dom, val, tp, oc, q)
def setup_inputs_ends(rng):
    tp, oc = graphs(rng)
    dom = 255 * (rng.random((N, 8, 16, NV)) < rng.random((N, 8, 1, NV))).astype(np.int64); val = 255 * (rng.random((N, 8, 16, NT)) < 0.3 * rng.random((N, 8, 1, NT))).astype(np.int64)
    dom[:, 1] = 0; val[:, 2] = 0; val[:, 3] = 255; dom[:, 5] = 255
    dom[:, 4] *= rng.random((N, 1, NV)) < 0.1; val[:, 6] *= rng.random((N, 1, NT)) < 0.1
    dom[:, 7] = rng.integers(240, 256, (N, 16, NV)); val[:, 7] = rng.integers(240, 256, (N, 16, NT))
    return pack(dom, val, tp, oc, rng.integers(0, NT, (N, 8, NL)))
def uneven(rng, n):
    return np.floor(np.exp2(8 * rng.random((N, 8, 1, n)) - 2 * rng.random((N, 8, 16, 1))) * rng.random((N, 8, 16, n))).astype(np.int64)
def setup_inputs_spread(rng):
    tp, oc = graphs(rng)
    return pack(uneven(rng, NV), uneven(rng, NT), tp, oc, np.minimum((NT * rng.random((N, 8, NL)) ** 3).astype(np.int64), NT - 1))
def check_inputs(d):
    bad = []
    for k, hi in (("dom", 255), ("val", 255), ("tp", NV - 1), ("oc", NT - 1), ("q", NT - 1)):
        v = np.asarray(d[k]).astype(np.float64)
        if not (np.all(v >= 0) and np.all(v <= hi) and np.all(v == np.floor(v))): bad.append("range of " + k)
    return bad
def pick(a, ix):
    return np.take_along_axis(a, ix[:, :, None, :], 3)
def reference(dom, val, tp, oc, q):
    dm = dom.astype(np.float32).astype(np.int64).reshape(N, 8, 16, NV); vl = val.astype(np.float32).astype(np.int64).reshape(N, 8, 16, NT)
    tpl = tp.astype(np.int64).reshape(N, 8, 16, NT); occ = oc.astype(np.int64).reshape(N, 8, 16, NV)
    cur = np.stack([gentries(a) for a in q]).astype(np.int64)
    for t in range(RO):
        p = pick(tpl, cur)
        x = pick(dm, p.reshape(N, 8, 16 * NL)).reshape(N, 8, 16, 16, NL)
        best = np.argmax(np.add.reduce(x, axis=2), axis=2)
        a = np.take_along_axis(p, best[:, :, None, :], 2)[:, :, 0]
        np.put_along_axis(vl, cur[:, :, None, :], np.min(x, axis=3), 3)
        p = pick(occ, a)
        x = pick(vl, p.reshape(N, 8, 16 * NL)).reshape(N, 8, 16, 16, NL)
        m = np.minimum(pick(dm, a), np.max(x, axis=3))
        best = np.argmax(np.add.reduce(x, axis=2), axis=2)
        cur = np.take_along_axis(p, best[:, :, None, :], 2)[:, :, 0]
        np.put_along_axis(dm, a[:, :, None, :], m, 3)
        d = 1 + t % (N - 1); ain = np.roll(a, d, axis=0); got = np.roll(m, d, axis=0)
        np.put_along_axis(dm, ain[:, :, None, :], np.minimum(pick(dm, ain), got), 3)
    s = np.stack([np.add.reduce(dm, axis=3), np.add.reduce(vl, axis=3)], axis=-1)
    return {"yt": cur.astype(np.float32), "yv": m.reshape(N, 128, NL).astype(np.float32).astype(BF), "ys": s.reshape(N, 128, 2).astype(np.float32)}

@@ -1,0 +1,417 @@
+from concourse.mybir import AluOpType as A, ActivationFunctionType as F
+
+NV, NT, NL, RO, PAD = 2048, 3072, 128, 4, 32
+OW = 16
+BIG = float(2 ** 25)
+PLAN1 = (4, (10, 14, 16))
+PLAN2 = (5, (11, 14, 16))
+SL = 768
+
+
+def sb(n, dtype):
+    return ("sbuf", [128, n], dtype)
+
+
+BF, F32, F16, U16, I32 = "bfloat16", "float32", "float16", "uint16", "int32"
+SCRATCH = {
+    "domS": sb(PAD + NV, BF), "valS": sb(PAD + NT, BF), "tpS": sb(NT, I32), "ocS": sb(NV, I32), "qS": sb(8, I32),
+    "xA": sb(PAD + NV, BF), "xB": sb(NV, BF), "wsA": sb(NV, BF), "wsB": sb(NV, BF),
+    "pA": sb(128, U16), "pB": sb(128, U16), "pm": sb(256, F16), "sA": sb(128, F16), "sB": sb(128, F16),
+    "mx": sb(128, F32), "ne": sb(128, F32), "yy": sb(256, F32), "dd": sb(256, F32),
+    "ou": sb(OW, U16), "oa": sb(RO * OW, U16), "ro": sb(RO * OW, U16), "mm": sb(RO * NL, BF), "rm": sb(RO * NL, BF),
+    "nw": sb(NL, BF), "win": sb(NL, BF), "fin": sb(132, F32), "basec": sb(4, F32), "junk": sb(128, F32), "ytS": sb(8, F32),
+    "pI": sb(4, I32), "cI": sb(4, I32), "cF": sb(4, F32), "mc": sb(4, F32),
+    "rowf": sb(144, F32), "dif": sb(128, F32), "r16": sb(128, F32), "b16": sb(128, F32),
+    "t1": sb(128, F32), "t2": sb(128, F32), "t3": sb(16, F32), "e1": sb(16, F32), "e2": sb(16, F32), "cc": sb(16, F32),
+    "Zl": sb(144, BF), "Ib": sb(128, BF), "tie": sb(128, BF), "Cb": sb(256, BF), "Z32": sb(256, BF),
+    "nI4": sb(128, F16), "Lh": sb(16 * 128, BF), "lane": sb(128, BF), "Xh": sb(128, F16), "Wh": sb(16 * 128, F16),
+    "Dm": sb(16, F16), "R01": sb(SL, BF), "ZB": sb(SL, BF),
+    "pK": ("psum", [128, 512], F32), "pP": ("psum", [128, 512], F32), "pD": ("psum", [128, 512], F32),
+    "pSV": ("psum", [128, 512], F32), "pSD": ("psum", [128, 512], F32),
+}
+SEMAPHORES = (["sent", "cv", "cs", "cp", "cg"] + ["aO%d" % t for t in range(RO)] + ["aM%d" % t for t in range(RO)]
+              + ["d%d" % i for i in range(8)])
+
+
+def schedule(ops, ext, eng, T):
+    writer, readers = dict(), dict()
+    for key in ext:
+        writer[key] = (("ext", key), 1, None)
+    know = {e: {} for e in eng}
+    clock = {}
+    count = {e: 0 for e in eng}
+    used = set()
+    plan = []
+    for q, call, reads, writes, grp in ops:
+        count[q] += 1
+        me = (("dma", count[q]), 1, None) if q == "y" else (q, count[q], grp)
+        need = {}
+        deps = [writer[k] for k in reads if k in writer]
+        for k in writes:
+            deps += ([writer[k]] if k in writer else []) + readers.get(k, [])
+        for src, n, gr in deps:
+            if src == q and grp is not None and gr == grp:
+                continue
+            need[src] = max(need.get(src, 0), n)
+        waits = []
+        for src in sorted(need, key=lambda a: -clock.get((a, need[a]), {}).get("at", 0)):
+            n = need[src]
+            if know[q].get(src, 0) >= n:
+                continue
+            waits.append((src, n))
+            used.add((src, n))
+            for a, b in clock.get((src, n), {}).items():
+                if a != "at":
+                    know[q][a] = max(know[q].get(a, 0), b)
+            know[q][src] = n
+        clock[me[:2]] = dict(know[q])
+        clock[me[:2]]["at"] = len(plan)
+        for k in reads:
+            readers.setdefault(k, []).append(me)
+        for k in writes:
+            writer[k] = me
+            readers[k] = []
+        plan.append((q, call, waits, me[:2]))
+    signal = {(("ext", key), 1): ext[key] for key in ext}
+    raised = {e: 0 for e in eng}
+    for q, call, waits, me in plan:
+        for d in waits:
+            eng[q].wait_ge(T.sem[signal[d][0]], signal[d][1])
+        if call is None:
+            continue
+        ins = call()
+        if me in used:
+            if q == "y":
+                signal[me] = ("d%d" % raised[q], 16)
+                raised[q] += 1
+            else:
+                raised[q] += 1
+                signal[me] = ("c" + q, raised[q])
+            ins.then_inc(T.sem[signal[me][0]], 16 if q == "y" else 1)
+
+
+def rank_program(g, core, T, topo):
+    rank = T.rank_of(core)
+    if rank is None:
+        return
+    n_ranks = len(T.cores)
+    V, S, P, Y = g.vector, g.scalar, g.tensor, g.sync
+    eng = {"v": V, "s": S, "p": P, "y": Y, "g": g}
+    ops = []
+
+    def op(q, call, reads, writes, grp=None):
+        ops.append((q, call, list(reads), list(writes), grp))
+
+    def ts(out, in0, s1, s2, o0, o1, reads, writes):
+        if o1 is None:
+            op("v", lambda: V.tensor_scalar(out, in0, s1, None, o0), reads, writes)
+        else:
+            op("v", lambda: V.tensor_scalar(out, in0, s1, s2, o0, o1), reads, writes)
+
+    def tt(out, in0, in1, o, reads, writes):
+        op("v", lambda: V.tensor_tensor(out, in0, in1, o), reads, writes)
+
+    def cp(out, in_, reads, writes):
+        op("v", lambda: V.tensor_copy(out, in_), reads, writes)
+
+    def ms(out, c, reads, writes):
+        op("v", lambda: V.memset(out, c), reads, writes)
+
+    def scan(out, d0, d1, init, o0, o1, reads, writes):
+        op("v", lambda: V.tensor_tensor_scan(out, d0, d1, init, o0, o1), reads, writes)
+
+    def mat(out, lhsT, rhs, start, stop, reads, writes, grp):
+        op("p", lambda: P.matmul(out, lhsT, rhs, start, stop), reads, writes, grp)
+
+    def iota(out, pattern, base, cm, key, flt=True):
+        if flt:
+            op("g", lambda: g.iota(out, pattern, base, cm, allow_small_or_imprecise_dtypes=True), [], [key])
+        else:
+            op("g", lambda: g.iota(out, pattern, base, cm), [], [key])
+
+    def dma(out, in_, reads, writes):
+        op("y", lambda: Y.dma_start(out, in_), reads, writes)
+
+    ext = {}
+    dests = []
+    for t in range(RO):
+        d = 1 + t % (n_ranks - 1)
+        dst = T.cores[(rank + d) % n_ranks]
+        src = T.cores[(rank - d) % n_ranks]
+        dests.append(dst)
+        got = len(topo.engines(src, core))
+        ext[("ro", t)] = ("aO%d" % t, got)
+        ext[("rm", t)] = ("aM%d" % t, got)
+    sent = [0]
+
+    def remote(t, out, in_, sem, reads):
+        dst = dests[t]
+        rid, pid = topo.addr(dst)[0], topo.addr(dst)[1]
+        mask = topo.mask(core, dst)
+        sent[0] += len(topo.engines(core, dst))
+        op("g", lambda: g.remote_dma(out, in_, T.sem[sem], T.sem.sent, pid, rid, mask), reads, [])
+
+    dma(T.qS[:], T.q[:], [], ["q"])
+    dma(T.tpS[:], T.tp[:], [], ["tp"])
+    dma(T.domS[:, PAD:], T.dom[:], [], ["dom"])
+    dma(T.valS[:, PAD:], T.val[:], [], ["val"])
+    dma(T.ocS[:], T.oc[:], [], ["oc"])
+
+    iota(T.pI[:, 0:1], [[0, 1]], 0, 1, "pI", False)
+    iota(T.dif[:], [[1, 128]], 0, -1, "dif")
+    iota(T.b16[:], [[16, 8], [0, 16]], 0, 0, "b16")
+    iota(T.r16[:], [[0, 8], [1, 16]], 0, 0, "r16")
+    iota(T.rowf[:], [[1, 144]], 0, 0, "rowf")
+    ms(T.Z32[:], 0.0, [], ["Z320"])
+    ms(T.ZB[:], 0.0, [], ["ZB0"])
+    ms(T.R01[:], 1.0, [], ["R0"])
+    ts(T.cI[:, 0:1], T.pI[:, 0:1], 15, None, A.bitwise_and, None, ["pI"], ["cI0"])
+    ts(T.cI[:, 1:2], T.pI[:, 0:1], 112, None, A.bitwise_and, None, ["pI"], ["cI1"])
+    ts(T.cI[:, 2:3], T.pI[:, 0:1], 16, None, A.bitwise_and, None, ["pI"], ["cI2"])
+    ms(T.ZB[:, 0:SL:16], 2.0 * BIG, ["ZB0"], ["ZB"])
+    ms(T.R01[:, 0:SL:16], 0.0, ["R0"], ["R01"])
+    ms(T.Z32[:, 0:256:32], 2.0 * BIG, ["Z320"], ["Z32"])
+    cp(T.cF[:, 0:3], T.cI[:, 0:3], ["cI0", "cI1", "cI2"], ["cF"])
+    rcol, gcol, hcol = T.cF[:, 0:1], T.cF[:, 1:2], T.cF[:, 2:3]
+    ts(T.Ib[:], T.dif[:], 0.0, None, A.is_equal, None, ["dif"], ["Ib"])
+    ts(T.Wh[:, 0:128], T.dif[:], 0.0, None, A.is_equal, None, ["dif"], [("W", 0)])
+    ts(T.t2[:], T.dif[:], 0.0, -8192.0, A.is_equal, A.mult, ["dif"], ["t2"])
+    ts(T.t1[:], T.b16[:], gcol, 4096.0, A.is_equal, A.mult, ["b16", "cF"], ["t1"])
+    ts(T.e1[:], T.r16[:, 0:16], rcol, None, A.is_equal, None, ["r16", "cF"], ["e1"])
+    for r in range(16):
+        op("s", lambda r=r: S.activation(T.Lh[:, 128 * r:128 * r + 128], T.t1[:], F.Identity, scale=T.e1[:, r:r + 1]),
+           ["t1", "e1"], [("L", r)])
+    ts(T.mc[:, 0:1], hcol, 0.0, None, A.is_equal, None, ["cF"], ["mc0"])
+    ts(T.mc[:, 1:2], hcol, 16.0, None, A.is_equal, None, ["cF"], ["mc1"])
+    tt(T.Xh[:], T.t1[:], T.t2[:], A.add, ["t1", "t2"], ["Xh"])
+    ts(T.cc[:], T.r16[:, 0:16], rcol, 4096.0, A.is_equal, A.mult, ["r16", "cF"], ["cc"])
+    ts(T.e2[:], T.r16[:, 0:16], 1.0, rcol, A.add, A.is_equal, ["r16", "cF"], ["e2"])
+    ts(T.t3[:], T.r16[:, 0:16], rcol, BIG, A.is_le, A.mult, ["r16", "cF"], ["t3"])
+    ts(T.cF[:, 3:4], rcol, 16.0, None, A.add, None, ["cF"], ["cF3"])
+    ts(T.tie[:], T.r16[:], -1.0 / 16, 15.0 / 16, A.mult, A.add, ["r16"], ["tie"])
+    ts(T.Zl[:], T.rowf[:], gcol, 15.0, A.subtract, A.is_equal, ["rowf", "cF"], ["Zl"])
+    ts(T.Cb[:, 0:16], T.t3[:], rcol, None, A.max, None, ["t3", "cF"], ["C0"])
+    ts(T.Cb[:, 16:32], T.t3[:], 0.0, rcol, A.mult, A.add, ["t3", "cF"], ["C1"])
+    ts(T.Cb[:, 32:48], T.t3[:], T.cF[:, 3:4], None, A.max, None, ["t3", "cF3"], ["C2"])
+    ms(T.Cb[:, 48:64], BIG, [], ["C3"])
+    tt(T.Dm[:], T.e1[:], T.e2[:], A.subtract, ["e1", "e2"], ["Dm"])
+    cp(T.Cb[:, 64:128], T.Cb[:, 0:64], ["C0", "C1", "C2", "C3"], ["C4"])
+    cp(T.ou[:, 0:8], T.qS[:], ["q"], ["uraw"])
+    cp(T.Cb[:, 128:256], T.Cb[:, 0:128], ["C0", "C1", "C2", "C3", "C4"], ["C5"])
+    ts(T.sB[:, 15:128:16], T.qS[:], -1024.0, None, A.add, None, ["q"], ["sB"])
+    ms(T.Cb[:, 0:256:32], 1024.0 + PAD, [], ["C0", "C2", "C4", "C5", "Cb"])
+    ts(T.nI4[:], T.dif[:], 0.0, -4096.0, A.is_equal, A.mult, ["dif"], ["nI4"])
+    for r in range(1, 16):
+        ts(T.Wh[:, 128 * r:128 * r + 128], T.Xh[:], T.cc[:, r:r + 1], None, A.min, None, ["Xh", "cc"], [("W", r)])
+
+    def twins(h, s, skey):
+        mat(T.pD[:, 0:256], T.Ib[:], T.Cb[:], True, False, ["Ib", "Cb"], ["pD"], ("D", h))
+        for r in range(16):
+            mat(T.pD[:, r:256:32], T.Wh[:, 128 * r:128 * r + 128], s[:, 15:128:16], False, False,
+                [("W", r), skey], ["pD"], ("D", h))
+        for r in range(16):
+            mat(T.pD[:, 16 + r:256:64], T.Lh[:, 128 * r:128 * r + 128], s[:, 31:128:32], False, False,
+                [("L", r), skey], ["pD"], ("D", h))
+        for r in range(16):
+            mat(T.pD[:, 16 + r:256:64], T.nI4[:], s[:, 15:128:32], False, r == 15, ["nI4", skey], ["pD"], ("D", h))
+
+    def absd():
+        op("s", lambda: S.activation(T.yy[:], T.pD[:, 0:256], F.Abs), ["pD"], ["yy"])
+
+    def ddscan():
+        scan(T.dd[:], T.Z32[:], T.yy[:], 0.0, A.add, A.min, ["Z32", "yy"], ["dd"])
+
+    def ddlist(buf, at, key):
+        cp(buf[:, at + 8:at + OW], T.dd[:, 31:256:32], ["dd"], [key])
+
+    def pointers(p, pkey, tab, tkey, lst, lkey):
+        cp(p[:], tab[:].indirect(lst), [tkey, lkey], [pkey])
+
+    def halves(p, pkey, e):
+        ts(T.pm[:, 128 * e:128 * e + 128], p[:], -1024.0, T.mc[:, e:e + 1], A.add, A.mult, [pkey, "mc%d" % e], [("pm", e)])
+
+    def turn(h):
+        for a in range(4):
+            for c in range(8):
+                mat(T.pP[32 * a:32 * a + 32, 16 * c:16 * c + 16], T.pm[32 * a:32 * a + 32, c:256:8],
+                    T.Dm[32 * a:32 * a + 32, :], True, True, [("pm", 0), ("pm", 1), "Dm"], ["pP"], ("P", h))
+
+    def kfirst(h):
+        mat(T.pK[:, 0:128], T.Ib[:], T.tie[:], True, False, ["Ib", "tie"], ["pK"], ("K", h))
+
+    def ksums(h, x, xn, k0, k1):
+        for k in range(k0, k1):
+            mat(T.pK[:, 0:128], T.Zl[:, 15 - k:143 - k], x[:, 128 * k:128 * k + 128], False, k == 15,
+                ["Zl", (xn, k)], ["pK"], ("K", h))
+
+    def total(ps, key, tab, tkey, n, out, okey):
+        for k in range(n // 128):
+            mat(ps[:, 0:128], T.Ib[:], tab[:, PAD + 128 * k:PAD + 128 * k + 128], k == 0, k == n // 128 - 1,
+                ["Ib", tkey], [key], key)
+        return lambda: op("s", lambda: S.activation(T.junk[:], ps[:, 0:128], F.Identity, accum_out=out), [key], ["junk", okey])
+
+    def gather(q, x, xn, tab, tkey, p, pkey, k0, k1):
+        src = tab[:, PAD:].indirect(p[:, 8 * k0:8 * k1])
+        out = x[:, 128 * k0:128 * k1]
+        keys = [(xn, k) for k in range(k0, k1)]
+        if q == "v":
+            cp(out, src, [tkey, pkey], keys)
+        else:
+            op("s", lambda: S.activation(out, src, F.Copy), [tkey, pkey], keys)
+
+    def fold(w, wn, x, xn, k0, k1, low):
+        n = 128 * (k1 - k0)
+        reads = [(xn, k) for k in range(k0, k1)]
+        keys = [(wn, k) for k in range(k0, k1)]
+        if low:
+            scan(w[:, 128 * k0:128 * k1], T.ZB[:, 0:n], x[:, 128 * k0:128 * k1], 0.0, A.add, A.min, reads + ["ZB"], keys)
+        else:
+            scan(w[:, 128 * k0:128 * k1], T.R01[:, 0:n], x[:, 128 * k0:128 * k1], 0.0, A.mult, A.max, reads + ["R01"], keys)
+
+    def best1():
+        scan(T.mx[:], T.R01[:, 0:128], T.pK[:, 0:128], 0.0, A.mult, A.max, ["R01", "pK"], ["mx"])
+
+    def best2():
+        tt(T.ne[:], T.pK[:, 0:128], T.mx[:], A.is_lt, ["pK", "mx"], ["ne"])
+
+    def best3(s, skey):
+        scan(s[:], T.ne[:], T.pP[:, 0:128], 0.0, A.mult, A.add, ["ne", "pP"], [skey])
+
+    def best4(out, s, skey, key):
+        ts(out, s[:, 15:128:16], 1024.0, None, A.add, None, [skey], [key])
+
+    def scat(tab, tkeys, lst, at, lkey, c, src, skeys):
+        cp(tab[:].indirect(lst[:, at + 8 + 2 * c:at + 10 + 2 * c]), src, [lkey] + skeys, tkeys)
+
+    kfirst("0a")
+    twins("0a", T.sB, "sB")
+    absd()
+    pointers(T.pA, "pA", T.tpS, "tp", T.ou[:, 0:8], "uraw")
+    ms(T.xA[:, NV:NV + PAD], 0.0, [], ["xpad"])
+    halves(T.pA, "pA", 0)
+    halves(T.pA, "pA", 1)
+    turn("0a")
+    cp(T.lane[:], T.rowf[:, 0:128], ["rowf"], ["lane"])
+
+    for t in range(RO):
+        ha, hb = "%da" % t, "%db" % t
+        at = OW * t
+        last = t == RO - 1
+        mt = T.mm[:, NL * t:NL * t + NL]
+        rmt = T.rm[:, NL * t:NL * t + NL]
+
+        def wsc(c):
+            scat(T.valS, ["val"], T.ou, 0, "udd", c, T.wsA[:, 512 * c + 15:512 * c + 512:16],
+                 [("wA", k) for k in range(4 * c, 4 * c + 4)])
+
+        def msc(c):
+            scat(T.domS, ["dom"], T.oa, at, ("add", t), c, T.mm[:, NL * t + 32 * c:NL * t + 32 * c + 32], [("m", t)])
+
+        nv, (e1, e2, e3) = PLAN1
+        gather("v", T.xA, "xA", T.domS, "dom", T.pA, "pA", 0, nv)
+        gather("s", T.xA, "xA", T.domS, "dom", T.pA, "pA", nv, e1)
+        gather("s", T.xA, "xA", T.domS, "dom", T.pA, "pA", e1, e2)
+        gather("s", T.xA, "xA", T.domS, "dom", T.pA, "pA", e2, e3)
+        ksums(ha, T.xA, "xA", 0, 16)
+        ddscan()
+        fold(T.wsA, "wA", T.xA, "xA", 0, nv, True)
+        ddlist(T.ou, 0, "udd")
+        fold(T.wsA, "wA", T.xA, "xA", nv, e1, True)
+        early = t > 0
+        if early:
+            wsc(0)
+        fold(T.wsA, "wA", T.xA, "xA", e1, e2, True)
+        if early:
+            wsc(1)
+        best1()
+        fold(T.wsA, "wA", T.xA, "xA", e2, e3, True)
+        best2()
+        wsc(2 if early else 0)
+        best3(T.sA, "sA")
+        wsc(3 if early else 1)
+        best4(T.oa[:, at:at + 8], T.sA, "sA", ("araw", t))
+        if not early:
+            wsc(2)
+            wsc(3)
+        pointers(T.pB, "pB", T.ocS, "oc", T.oa[:, at:at + 8], ("araw", t))
+
+        nv, (e1, e2, e3) = PLAN2
+        twins(hb, T.sA, "sA")
+        kfirst(hb)
+        if last:
+            sumv = total(T.pSV, "pSV", T.valS, "val", NT, T.fin[:, 128:129], "sumv")
+        gather("v", T.xB, "xB", T.valS, "val", T.pB, "pB", 0, nv)
+        gather("s", T.xB, "xB", T.valS, "val", T.pB, "pB", nv, e1)
+        absd()
+        gather("s", T.xB, "xB", T.valS, "val", T.pB, "pB", e1, e2)
+        gather("s", T.xB, "xB", T.valS, "val", T.pB, "pB", e2, e3)
+        ksums(hb, T.xB, "xB", 0, 16)
+        halves(T.pB, "pB", 0)
+        fold(T.wsB, "wB", T.xB, "xB", 0, nv, False)
+        fold(T.wsB, "wB", T.xB, "xB", nv, e1, False)
+        ddscan()
+        halves(T.pB, "pB", 1)
+        turn(hb)
+        ddlist(T.oa, at, ("add", t))
+        remote(t, T.ro[:, at:at + OW], T.oa[:, at:at + OW], "aO%d" % t, [("araw", t), ("add", t)])
+        fold(T.wsB, "wB", T.xB, "xB", e1, e2, False)
+        fold(T.wsB, "wB", T.xB, "xB", e2, e3, False)
+        tt(mt, T.domS[:, PAD:].indirect(T.oa[:, at:at + 8]), T.wsB[:, 15:NV:16], A.min,
+           ["dom", ("araw", t)] + [("wB", k) for k in range(16)], [("m", t)])
+        remote(t, rmt, mt, "aM%d" % t, [("m", t)])
+
+        if not last:
+            hn = "%da" % (t + 1)
+            best1()
+            msc(0)
+            best2()
+            msc(1)
+            best3(T.sB, "sB")
+            msc(2)
+            best4(T.ou[:, 0:8], T.sB, "sB", "uraw")
+            kfirst(hn)
+            twins(hn, T.sB, "sB")
+            absd()
+            msc(3)
+            pointers(T.pA, "pA", T.tpS, "tp", T.ou[:, 0:8], "uraw")
+
+            def rsc(c):
+                scat(T.domS, ["dom"], T.ro, at, ("ro", t), c, T.nw[:, 32 * c:32 * c + 32], ["nw"])
+
+            tt(T.nw[:], T.domS[:, PAD:].indirect(T.ro[:, at:at + 8]), rmt, A.min, ["dom", ("ro", t), ("rm", t)], ["nw"])
+            rsc(0)
+            halves(T.pA, "pA", 0)
+            rsc(1)
+            halves(T.pA, "pA", 1)
+            rsc(2)
+            rsc(3)
+            turn(hn)
+        else:
+            tag = [("xA", k) for k in range(16)] + ["xpad"]
+
+            def mark(c):
+                scat(T.xA, tag, T.ro, at, ("ro", t), c, T.lane[:, 32 * c:32 * c + 32], ["lane"])
+
+            dma(T.yv[:], mt, [("m", t)], ["yv"])
+            sumv()
+            for c in range(4):
+                msc(c)
+            total(T.pSD, "pSD", T.domS, "dom", NV, T.basec[:, 0:1], "base")()
+            mark(0)
+            best1()
+            mark(1)
+            best2()
+            mark(2)
+            best3(T.sB, "sB")
+            mark(3)
+            best4(T.ytS[:], T.sB, "sB", "ytS")
+            dma(T.yt[:], T.ytS[:], ["ytS"], ["yt"])
+            tt(T.win[:], T.xA[:, PAD:].indirect(T.ro[:, at:at + 8]), T.lane[:], A.is_equal, tag + ["lane", ("ro", t)], ["win"])
+            tt(T.nw[:], T.domS[:, PAD:].indirect(T.ro[:, at:at + 8]), T.win[:], A.mult, ["dom", "win", ("ro", t)], ["nw"])
+            tt(T.win[:], T.nw[:], rmt, A.min, ["nw", ("rm", t)], ["win"])
+            scan(T.fin[:, 0:128], T.win[:], T.nw[:], T.basec[:, 0:1], A.add, A.subtract, ["win", "nw", "base"], ["fin"])
+            dma(T.ys[:], T.fin[:, 127:129], ["fin", "sumv"], ["ys"])
+
+    op("y", None, ["yv", "yt", "ys"], [])
+    schedule(ops, ext, eng, T)
+    g.wait_ge(T.sem.sent, sent[0])

@@ -3,8 +3,8 @@ from concourse.mybir import AluOpType as A, ActivationFunctionType as F
 NV, NT, NL, RO, PAD = 2048, 3072, 128, 4, 32
 OW = 16
 BIG = float(2 ** 25)
-PLAN1 = (4, (10, 14, 16))
-PLAN2 = (5, (11, 14, 16))
+PLAN1 = (5, (11, 15, 16))
+PLAN2 = (5, (11, 15, 16))
 SL = 768
 
 
@@ -20,16 +20,17 @@ SCRATCH = {
     "mx": sb(128, F32), "ne": sb(128, F32), "yy": sb(256, F32), "dd": sb(256, F32),
     "ou": sb(OW, U16), "oa": sb(RO * OW, U16), "ro": sb(RO * OW, U16), "mm": sb(RO * NL, BF), "rm": sb(RO * NL, BF),
     "nw": sb(NL, BF), "win": sb(NL, BF), "fin": sb(132, F32), "basec": sb(4, F32), "junk": sb(128, F32), "ytS": sb(8, F32),
+    "wide": sb(NT, BF),
     "pI": sb(4, I32), "cI": sb(4, I32), "cF": sb(4, F32), "mc": sb(4, F32),
     "rowf": sb(144, F32), "dif": sb(128, F32), "r16": sb(128, F32), "b16": sb(128, F32),
-    "t1": sb(128, F32), "t2": sb(128, F32), "t3": sb(16, F32), "e1": sb(16, F32), "e2": sb(16, F32), "cc": sb(16, F32),
+    "t1": sb(128, F32), "t3": sb(16, F32), "e1": sb(16, F32), "e2": sb(16, F32),
     "Zl": sb(144, BF), "Ib": sb(128, BF), "tie": sb(128, BF), "Cb": sb(256, BF), "Z32": sb(256, BF),
-    "nI4": sb(128, F16), "Lh": sb(16 * 128, BF), "lane": sb(128, BF), "Xh": sb(128, F16), "Wh": sb(16 * 128, F16),
+    "nI4": sb(128, BF), "Lh": sb(16 * 128, BF), "lane": sb(128, BF), "Wh": sb(16 * 128, BF),
     "Dm": sb(16, F16), "R01": sb(SL, BF), "ZB": sb(SL, BF),
     "pK": ("psum", [128, 512], F32), "pP": ("psum", [128, 512], F32), "pD": ("psum", [128, 512], F32),
-    "pSV": ("psum", [128, 512], F32), "pSD": ("psum", [128, 512], F32),
+    "pSD": ("psum", [128, 512], F32),
 }
-SEMAPHORES = (["sent", "cv", "cs", "cp", "cg"] + ["aO%d" % t for t in range(RO)] + ["aM%d" % t for t in range(RO)]
+SEMAPHORES = (["sent", "cv", "cs", "cp", "cg", "aR"] + ["aA%d" % t for t in range(RO)] + ["aB%d" % t for t in range(RO)]
               + ["d%d" % i for i in range(8)])
 
 
@@ -140,8 +141,10 @@ def rank_program(g, core, T, topo):
         src = T.cores[(rank - d) % n_ranks]
         dests.append(dst)
         got = len(topo.engines(src, core))
-        ext[("ro", t)] = ("aO%d" % t, got)
-        ext[("rm", t)] = ("aM%d" % t, got)
+        ext[("rA", t)] = ("aA%d" % t, got)
+        ext[("rB", t)] = ("aB%d" % t, got)
+        if t == 0:
+            ext["rR"] = ("aR", got)
     sent = [0]
 
     def remote(t, out, in_, sem, reads):
@@ -158,33 +161,34 @@ def rank_program(g, core, T, topo):
     dma(T.ocS[:], T.oc[:], [], ["oc"])
 
     iota(T.pI[:, 0:1], [[0, 1]], 0, 1, "pI", False)
-    iota(T.dif[:], [[1, 128]], 0, -1, "dif")
     iota(T.b16[:], [[16, 8], [0, 16]], 0, 0, "b16")
     iota(T.r16[:], [[0, 8], [1, 16]], 0, 0, "r16")
+    iota(T.dif[:], [[1, 128]], 0, -1, "dif")
     iota(T.rowf[:], [[1, 144]], 0, 0, "rowf")
     ms(T.Z32[:], 0.0, [], ["Z320"])
-    ms(T.ZB[:], 0.0, [], ["ZB0"])
-    ms(T.R01[:], 1.0, [], ["R0"])
     ts(T.cI[:, 0:1], T.pI[:, 0:1], 15, None, A.bitwise_and, None, ["pI"], ["cI0"])
     ts(T.cI[:, 1:2], T.pI[:, 0:1], 112, None, A.bitwise_and, None, ["pI"], ["cI1"])
     ts(T.cI[:, 2:3], T.pI[:, 0:1], 16, None, A.bitwise_and, None, ["pI"], ["cI2"])
-    ms(T.ZB[:, 0:SL:16], 2.0 * BIG, ["ZB0"], ["ZB"])
-    ms(T.R01[:, 0:SL:16], 0.0, ["R0"], ["R01"])
     ms(T.Z32[:, 0:256:32], 2.0 * BIG, ["Z320"], ["Z32"])
     cp(T.cF[:, 0:3], T.cI[:, 0:3], ["cI0", "cI1", "cI2"], ["cF"])
     rcol, gcol, hcol = T.cF[:, 0:1], T.cF[:, 1:2], T.cF[:, 2:3]
-    ts(T.Ib[:], T.dif[:], 0.0, None, A.is_equal, None, ["dif"], ["Ib"])
-    ts(T.Wh[:, 0:128], T.dif[:], 0.0, None, A.is_equal, None, ["dif"], [("W", 0)])
-    ts(T.t2[:], T.dif[:], 0.0, -8192.0, A.is_equal, A.mult, ["dif"], ["t2"])
+    ms(T.Cb[:, 48:64], BIG, [], ["C3"])
     ts(T.t1[:], T.b16[:], gcol, 4096.0, A.is_equal, A.mult, ["b16", "cF"], ["t1"])
     ts(T.e1[:], T.r16[:, 0:16], rcol, None, A.is_equal, None, ["r16", "cF"], ["e1"])
-    for r in range(16):
+    for r in list(range(1, 16)) + [0]:
         op("s", lambda r=r: S.activation(T.Lh[:, 128 * r:128 * r + 128], T.t1[:], F.Identity, scale=T.e1[:, r:r + 1]),
            ["t1", "e1"], [("L", r)])
+    for r0 in (1, 6, 11):
+        op("g", lambda r0=r0: g.affine_select(T.Wh[:, 128 * r0:128 * r0 + 640], T.Lh[:, 128 * r0:128 * r0 + 640],
+                                              [[0, 5], [1, 128]], A.not_equal, -4096.0, 0, -1),
+           [("L", r) for r in range(r0, r0 + 5)], [("W", r) for r in range(r0, r0 + 5)])
+    ms(T.ZB[:], 0.0, [], ["ZB0"])
+    ms(T.R01[:], 1.0, [], ["R0"])
+    ms(T.ZB[:, 0:SL:16], 2.0 * BIG, ["ZB0"], ["ZB"])
+    ms(T.R01[:, 0:SL:16], 0.0, ["R0"], ["R01"])
+    ts(T.Ib[:], T.dif[:], 0.0, None, A.is_equal, None, ["dif"], ["Ib"])
     ts(T.mc[:, 0:1], hcol, 0.0, None, A.is_equal, None, ["cF"], ["mc0"])
     ts(T.mc[:, 1:2], hcol, 16.0, None, A.is_equal, None, ["cF"], ["mc1"])
-    tt(T.Xh[:], T.t1[:], T.t2[:], A.add, ["t1", "t2"], ["Xh"])
-    ts(T.cc[:], T.r16[:, 0:16], rcol, 4096.0, A.is_equal, A.mult, ["r16", "cF"], ["cc"])
     ts(T.e2[:], T.r16[:, 0:16], 1.0, rcol, A.add, A.is_equal, ["r16", "cF"], ["e2"])
     ts(T.t3[:], T.r16[:, 0:16], rcol, BIG, A.is_le, A.mult, ["r16", "cF"], ["t3"])
     ts(T.cF[:, 3:4], rcol, 16.0, None, A.add, None, ["cF"], ["cF3"])
@@ -193,7 +197,6 @@ def rank_program(g, core, T, topo):
     ts(T.Cb[:, 0:16], T.t3[:], rcol, None, A.max, None, ["t3", "cF"], ["C0"])
     ts(T.Cb[:, 16:32], T.t3[:], 0.0, rcol, A.mult, A.add, ["t3", "cF"], ["C1"])
     ts(T.Cb[:, 32:48], T.t3[:], T.cF[:, 3:4], None, A.max, None, ["t3", "cF3"], ["C2"])
-    ms(T.Cb[:, 48:64], BIG, [], ["C3"])
     tt(T.Dm[:], T.e1[:], T.e2[:], A.subtract, ["e1", "e2"], ["Dm"])
     cp(T.Cb[:, 64:128], T.Cb[:, 0:64], ["C0", "C1", "C2", "C3"], ["C4"])
     cp(T.ou[:, 0:8], T.qS[:], ["q"], ["uraw"])
@@ -201,19 +204,21 @@ def rank_program(g, core, T, topo):
     ts(T.sB[:, 15:128:16], T.qS[:], -1024.0, None, A.add, None, ["q"], ["sB"])
     ms(T.Cb[:, 0:256:32], 1024.0 + PAD, [], ["C0", "C2", "C4", "C5", "Cb"])
     ts(T.nI4[:], T.dif[:], 0.0, -4096.0, A.is_equal, A.mult, ["dif"], ["nI4"])
-    for r in range(1, 16):
-        ts(T.Wh[:, 128 * r:128 * r + 128], T.Xh[:], T.cc[:, r:r + 1], None, A.min, None, ["Xh", "cc"], [("W", r)])
+    ms(T.xA[:, NV:NV + PAD], 0.0, [], ["xpad"])
+    cp(T.lane[:], T.rowf[:, 0:128], ["rowf"], ["lane"])
 
-    def twins(h, s, skey):
-        mat(T.pD[:, 0:256], T.Ib[:], T.Cb[:], True, False, ["Ib", "Cb"], ["pD"], ("D", h))
-        for r in range(16):
-            mat(T.pD[:, r:256:32], T.Wh[:, 128 * r:128 * r + 128], s[:, 15:128:16], False, False,
-                [("W", r), skey], ["pD"], ("D", h))
-        for r in range(16):
-            mat(T.pD[:, 16 + r:256:64], T.Lh[:, 128 * r:128 * r + 128], s[:, 31:128:32], False, False,
-                [("L", r), skey], ["pD"], ("D", h))
-        for r in range(16):
-            mat(T.pD[:, 16 + r:256:64], T.nI4[:], s[:, 15:128:32], False, r == 15, ["nI4", skey], ["pD"], ("D", h))
+    def twins(h, s, skey, parts=(0, 1)):
+        if 0 in parts:
+            mat(T.pD[:, 0:256], T.Ib[:], T.Cb[:], True, False, ["Ib", "Cb"], ["pD"], ("D", h))
+            for r in range(16):
+                mat(T.pD[:, 16 + r:256:64], T.nI4[:], s[:, 15:128:32], False, False, ["nI4", skey], ["pD"], ("D", h))
+            for r in range(16):
+                mat(T.pD[:, 16 + r:256:64], T.Lh[:, 128 * r:128 * r + 128], s[:, 31:128:32], False, False,
+                    [("L", r), skey], ["pD"], ("D", h))
+        if 1 in parts:
+            for r in range(16):
+                mat(T.pD[:, r:256:32], T.Wh[:, 128 * r:128 * r + 128] if r else T.Ib[:], s[:, 15:128:16], False, r == 15,
+                    [("W", r), skey], ["pD"], ("D", h))
 
     def absd():
         op("s", lambda: S.activation(T.yy[:], T.pD[:, 0:256], F.Abs), ["pD"], ["yy"])
@@ -221,8 +226,8 @@ def rank_program(g, core, T, topo):
     def ddscan():
         scan(T.dd[:], T.Z32[:], T.yy[:], 0.0, A.add, A.min, ["Z32", "yy"], ["dd"])
 
-    def ddlist(buf, at, key):
-        cp(buf[:, at + 8:at + OW], T.dd[:, 31:256:32], ["dd"], [key])
+    def ddlist(buf, key):
+        cp(buf[:, 8:OW], T.dd[:, 31:256:32], ["dd"], [key])
 
     def pointers(p, pkey, tab, tkey, lst, lkey):
         cp(p[:], tab[:].indirect(lst), [tkey, lkey], [pkey])
@@ -248,7 +253,7 @@ def rank_program(g, core, T, topo):
         for k in range(n // 128):
             mat(ps[:, 0:128], T.Ib[:], tab[:, PAD + 128 * k:PAD + 128 * k + 128], k == 0, k == n // 128 - 1,
                 ["Ib", tkey], [key], key)
-        return lambda: op("s", lambda: S.activation(T.junk[:], ps[:, 0:128], F.Identity, accum_out=out), [key], ["junk", okey])
+        op("s", lambda: S.activation(T.junk[:], ps[:, 0:128], F.Identity, accum_out=out), [key], ["junk", okey])
 
     def gather(q, x, xn, tab, tkey, p, pkey, k0, k1):
         src = tab[:, PAD:].indirect(p[:, 8 * k0:8 * k1])
@@ -280,66 +285,83 @@ def rank_program(g, core, T, topo):
     def best4(out, s, skey, key):
         ts(out, s[:, 15:128:16], 1024.0, None, A.add, None, [skey], [key])
 
-    def scat(tab, tkeys, lst, at, lkey, c, src, skeys):
-        cp(tab[:].indirect(lst[:, at + 8 + 2 * c:at + 10 + 2 * c]), src, [lkey] + skeys, tkeys)
+    def scat(tab, tkeys, lst, lkey, c, src, skeys):
+        cp(tab[:].indirect(lst[:, 8 + 2 * c:10 + 2 * c]), src, [lkey] + skeys, tkeys)
 
     kfirst("0a")
-    twins("0a", T.sB, "sB")
-    absd()
+    twins("0a", T.sB, "sB", (0,))
     pointers(T.pA, "pA", T.tpS, "tp", T.ou[:, 0:8], "uraw")
-    ms(T.xA[:, NV:NV + PAD], 0.0, [], ["xpad"])
     halves(T.pA, "pA", 0)
     halves(T.pA, "pA", 1)
     turn("0a")
-    cp(T.lane[:], T.rowf[:, 0:128], ["rowf"], ["lane"])
 
     for t in range(RO):
         ha, hb = "%da" % t, "%db" % t
-        at = OW * t
-        last = t == RO - 1
+        first, last = t == 0, t == RO - 1
         mt = T.mm[:, NL * t:NL * t + NL]
         rmt = T.rm[:, NL * t:NL * t + NL]
+        rk = ("rA", t)
+
+        def lst(buf, c0, c1):
+            return buf[:, OW * t + c0:OW * t + c1]
+
+        def put(tab, tkeys, buf, lkey, c, src, skeys):
+            cp(tab[:].indirect(lst(buf, 8 + 2 * c, 10 + 2 * c)), src, [lkey] + skeys, tkeys)
 
         def wsc(c):
-            scat(T.valS, ["val"], T.ou, 0, "udd", c, T.wsA[:, 512 * c + 15:512 * c + 512:16],
+            scat(T.valS, ["val"], T.ou, "udd", c, T.wsA[:, 512 * c + 15:512 * c + 512:16],
                  [("wA", k) for k in range(4 * c, 4 * c + 4)])
 
         def msc(c):
-            scat(T.domS, ["dom"], T.oa, at, ("add", t), c, T.mm[:, NL * t + 32 * c:NL * t + 32 * c + 32], [("m", t)])
+            put(T.domS, ["dom"], T.oa, ("add", t), c, T.mm[:, NL * t + 32 * c:NL * t + 32 * c + 32], [("m", t)])
 
         nv, (e1, e2, e3) = PLAN1
         gather("v", T.xA, "xA", T.domS, "dom", T.pA, "pA", 0, nv)
         gather("s", T.xA, "xA", T.domS, "dom", T.pA, "pA", nv, e1)
         gather("s", T.xA, "xA", T.domS, "dom", T.pA, "pA", e1, e2)
         gather("s", T.xA, "xA", T.domS, "dom", T.pA, "pA", e2, e3)
-        ksums(ha, T.xA, "xA", 0, 16)
-        ddscan()
-        fold(T.wsA, "wA", T.xA, "xA", 0, nv, True)
-        ddlist(T.ou, 0, "udd")
-        fold(T.wsA, "wA", T.xA, "xA", nv, e1, True)
-        early = t > 0
-        if early:
+        if first:
+            ksums(ha, T.xA, "xA", 0, nv)
+            twins(ha, T.sB, "sB", (1,))
+            ksums(ha, T.xA, "xA", nv, 16)
+            absd()
+            fold(T.wsA, "wA", T.xA, "xA", 0, nv, True)
+            fold(T.wsA, "wA", T.xA, "xA", nv, e1, True)
+            fold(T.wsA, "wA", T.xA, "xA", e1, e2, True)
+            best1()
+            ddscan()
+            best2()
+            ddlist(T.ou, "udd")
+            best3(T.sA, "sA")
             wsc(0)
-        fold(T.wsA, "wA", T.xA, "xA", e1, e2, True)
-        if early:
+            best4(lst(T.oa, 0, 8), T.sA, "sA", ("araw", t))
+            remote(t, lst(T.ro, 0, 8), lst(T.oa, 0, 8), "aR", [("araw", t), "oc"])
             wsc(1)
-        best1()
-        fold(T.wsA, "wA", T.xA, "xA", e2, e3, True)
-        best2()
-        wsc(2 if early else 0)
-        best3(T.sA, "sA")
-        wsc(3 if early else 1)
-        best4(T.oa[:, at:at + 8], T.sA, "sA", ("araw", t))
-        if not early:
+            fold(T.wsA, "wA", T.xA, "xA", e2, e3, True)
             wsc(2)
             wsc(3)
-        pointers(T.pB, "pB", T.ocS, "oc", T.oa[:, at:at + 8], ("araw", t))
+            pointers(T.pB, "pB", T.ocS, "oc", lst(T.oa, 0, 8), ("araw", t))
+        else:
+            ksums(ha, T.xA, "xA", 0, 16)
+            ddscan()
+            fold(T.wsA, "wA", T.xA, "xA", 0, nv, True)
+            ddlist(T.ou, "udd")
+            fold(T.wsA, "wA", T.xA, "xA", nv, e1, True)
+            wsc(0)
+            fold(T.wsA, "wA", T.xA, "xA", e1, e2, True)
+            best1()
+            fold(T.wsA, "wA", T.xA, "xA", e2, e3, True)
+            best2()
+            wsc(1)
+            best3(T.sA, "sA")
+            wsc(2)
+            best4(lst(T.oa, 0, 8), T.sA, "sA", ("araw", t))
+            wsc(3)
+            pointers(T.pB, "pB", T.ocS, "oc", lst(T.oa, 0, 8), ("araw", t))
 
         nv, (e1, e2, e3) = PLAN2
         twins(hb, T.sA, "sA")
         kfirst(hb)
-        if last:
-            sumv = total(T.pSV, "pSV", T.valS, "val", NT, T.fin[:, 128:129], "sumv")
         gather("v", T.xB, "xB", T.valS, "val", T.pB, "pB", 0, nv)
         gather("s", T.xB, "xB", T.valS, "val", T.pB, "pB", nv, e1)
         absd()
@@ -352,13 +374,14 @@ def rank_program(g, core, T, topo):
         ddscan()
         halves(T.pB, "pB", 1)
         turn(hb)
-        ddlist(T.oa, at, ("add", t))
-        remote(t, T.ro[:, at:at + OW], T.oa[:, at:at + OW], "aO%d" % t, [("araw", t), ("add", t)])
+        ddlist(T.oa[:, OW * t:OW * t + OW], ("add", t))
+        c0 = 8 if first else 0
+        remote(t, lst(T.ro, c0, OW), lst(T.oa, c0, OW), "aA%d" % t, [("araw", t), ("add", t)])
         fold(T.wsB, "wB", T.xB, "xB", e1, e2, False)
         fold(T.wsB, "wB", T.xB, "xB", e2, e3, False)
-        tt(mt, T.domS[:, PAD:].indirect(T.oa[:, at:at + 8]), T.wsB[:, 15:NV:16], A.min,
+        tt(mt, T.domS[:, PAD:].indirect(lst(T.oa, 0, 8)), T.wsB[:, 15:NV:16], A.min,
            ["dom", ("araw", t)] + [("wB", k) for k in range(16)], [("m", t)])
-        remote(t, rmt, mt, "aM%d" % t, [("m", t)])
+        remote(t, rmt, mt, "aB%d" % t, [("m", t)])
 
         if not last:
             hn = "%da" % (t + 1)
@@ -376,9 +399,10 @@ def rank_program(g, core, T, topo):
             pointers(T.pA, "pA", T.tpS, "tp", T.ou[:, 0:8], "uraw")
 
             def rsc(c):
-                scat(T.domS, ["dom"], T.ro, at, ("ro", t), c, T.nw[:, 32 * c:32 * c + 32], ["nw"])
+                put(T.domS, ["dom"], T.ro, rk, c, T.nw[:, 32 * c:32 * c + 32], ["nw"])
 
-            tt(T.nw[:], T.domS[:, PAD:].indirect(T.ro[:, at:at + 8]), rmt, A.min, ["dom", ("ro", t), ("rm", t)], ["nw"])
+            tt(T.nw[:], T.domS[:, PAD:].indirect(lst(T.ro, 0, 8)), rmt, A.min,
+               ["dom", rk, ("rB", t)] + (["rR"] if first else []), ["nw"])
             rsc(0)
             halves(T.pA, "pA", 0)
             rsc(1)
@@ -390,25 +414,28 @@ def rank_program(g, core, T, topo):
             tag = [("xA", k) for k in range(16)] + ["xpad"]
 
             def mark(c):
-                scat(T.xA, tag, T.ro, at, ("ro", t), c, T.lane[:, 32 * c:32 * c + 32], ["lane"])
+                put(T.xA, tag, T.ro, rk, c, T.lane[:, 32 * c:32 * c + 32], ["lane"])
 
             dma(T.yv[:], mt, [("m", t)], ["yv"])
-            sumv()
-            for c in range(4):
-                msc(c)
-            total(T.pSD, "pSD", T.domS, "dom", NV, T.basec[:, 0:1], "base")()
-            mark(0)
+            op("s", lambda: S.activation(T.wide[:], T.valS[:, PAD:], F.Identity, accum_out=T.fin[:, 128:129]),
+               ["val"], ["sumv"])
             best1()
-            mark(1)
+            msc(0)
             best2()
+            msc(1)
+            mark(0)
+            msc(2)
+            mark(1)
+            msc(3)
+            total(T.pSD, "pSD", T.domS, "dom", NV, T.basec[:, 0:1], "base")
             mark(2)
             best3(T.sB, "sB")
             mark(3)
             best4(T.ytS[:], T.sB, "sB", "ytS")
             dma(T.yt[:], T.ytS[:], ["ytS"], ["yt"])
-            tt(T.win[:], T.xA[:, PAD:].indirect(T.ro[:, at:at + 8]), T.lane[:], A.is_equal, tag + ["lane", ("ro", t)], ["win"])
-            tt(T.nw[:], T.domS[:, PAD:].indirect(T.ro[:, at:at + 8]), T.win[:], A.mult, ["dom", "win", ("ro", t)], ["nw"])
-            tt(T.win[:], T.nw[:], rmt, A.min, ["nw", ("rm", t)], ["win"])
+            tt(T.win[:], T.xA[:, PAD:].indirect(lst(T.ro, 0, 8)), T.lane[:], A.is_equal, tag + ["lane", rk], ["win"])
+            tt(T.nw[:], T.domS[:, PAD:].indirect(lst(T.ro, 0, 8)), T.win[:], A.mult, ["dom", "win", rk], ["nw"])
+            tt(T.win[:], T.nw[:], rmt, A.min, ["nw", ("rB", t)], ["win"])
             scan(T.fin[:, 0:128], T.win[:], T.nw[:], T.basec[:, 0:1], A.add, A.subtract, ["win", "nw", "base"], ["fin"])
             dma(T.ys[:], T.fin[:, 127:129], ["fin", "sumv"], ["ys"])
 

from concourse.mybir import AluOpType as A, ActivationFunctionType as F

NV, NT, NL, RO, PAD = 2048, 3072, 128, 4, 32
OW = 16
BIG = float(2 ** 25)
PLAN1 = (5, (11, 15, 16))
PLAN2 = (5, (11, 15, 16))
SL = 768


def sb(n, dtype):
    return ("sbuf", [128, n], dtype)


BF, F32, F16, U16, I32 = "bfloat16", "float32", "float16", "uint16", "int32"
SCRATCH = {
    "domS": sb(PAD + NV, BF), "valS": sb(PAD + NT, BF), "tpS": sb(NT, I32), "ocS": sb(NV, I32), "qS": sb(8, I32),
    "xA": sb(PAD + NV, BF), "xB": sb(NV, BF), "wsA": sb(NV, BF), "wsB": sb(NV, BF),
    "pA": sb(128, U16), "pB": sb(128, U16), "pm": sb(256, F16), "sA": sb(128, F16), "sB": sb(128, F16),
    "mx": sb(128, F32), "ne": sb(128, F32), "yy": sb(256, F32), "dd": sb(256, F32),
    "ou": sb(OW, U16), "oa": sb(RO * OW, U16), "ro": sb(RO * OW, U16), "mm": sb(RO * NL, BF), "rm": sb(RO * NL, BF),
    "nw": sb(NL, BF), "win": sb(NL, BF), "fin": sb(132, F32), "basec": sb(4, F32), "junk": sb(128, F32), "ytS": sb(8, F32),
    "wide": sb(NT, BF),
    "pI": sb(4, I32), "cI": sb(4, I32), "cF": sb(4, F32), "mc": sb(4, F32),
    "rowf": sb(144, F32), "dif": sb(128, F32), "r16": sb(128, F32), "b16": sb(128, F32),
    "t1": sb(128, F32), "t3": sb(16, F32), "e1": sb(16, F32), "e2": sb(16, F32),
    "Zl": sb(144, BF), "Ib": sb(128, BF), "tie": sb(128, BF), "Cb": sb(256, BF), "Z32": sb(256, BF),
    "nI4": sb(128, BF), "Lh": sb(16 * 128, BF), "lane": sb(128, BF), "Wh": sb(16 * 128, BF),
    "Dm": sb(16, F16), "R01": sb(SL, BF), "ZB": sb(SL, BF),
    "pK": ("psum", [128, 512], F32), "pP": ("psum", [128, 512], F32), "pD": ("psum", [128, 512], F32),
    "pSD": ("psum", [128, 512], F32),
}
SEMAPHORES = (["sent", "cv", "cs", "cp", "cg", "aR"] + ["aA%d" % t for t in range(RO)] + ["aB%d" % t for t in range(RO)]
              + ["d%d" % i for i in range(8)])


def schedule(ops, ext, eng, T):
    writer, readers = dict(), dict()
    for key in ext:
        writer[key] = (("ext", key), 1, None)
    know = {e: {} for e in eng}
    clock = {}
    count = {e: 0 for e in eng}
    used = set()
    plan = []
    for q, call, reads, writes, grp in ops:
        count[q] += 1
        me = (("dma", count[q]), 1, None) if q == "y" else (q, count[q], grp)
        need = {}
        deps = [writer[k] for k in reads if k in writer]
        for k in writes:
            deps += ([writer[k]] if k in writer else []) + readers.get(k, [])
        for src, n, gr in deps:
            if src == q and grp is not None and gr == grp:
                continue
            need[src] = max(need.get(src, 0), n)
        waits = []
        for src in sorted(need, key=lambda a: -clock.get((a, need[a]), {}).get("at", 0)):
            n = need[src]
            if know[q].get(src, 0) >= n:
                continue
            waits.append((src, n))
            used.add((src, n))
            for a, b in clock.get((src, n), {}).items():
                if a != "at":
                    know[q][a] = max(know[q].get(a, 0), b)
            know[q][src] = n
        clock[me[:2]] = dict(know[q])
        clock[me[:2]]["at"] = len(plan)
        for k in reads:
            readers.setdefault(k, []).append(me)
        for k in writes:
            writer[k] = me
            readers[k] = []
        plan.append((q, call, waits, me[:2]))
    signal = {(("ext", key), 1): ext[key] for key in ext}
    raised = {e: 0 for e in eng}
    for q, call, waits, me in plan:
        for d in waits:
            eng[q].wait_ge(T.sem[signal[d][0]], signal[d][1])
        if call is None:
            continue
        ins = call()
        if me in used:
            if q == "y":
                signal[me] = ("d%d" % raised[q], 16)
                raised[q] += 1
            else:
                raised[q] += 1
                signal[me] = ("c" + q, raised[q])
            ins.then_inc(T.sem[signal[me][0]], 16 if q == "y" else 1)


def rank_program(g, core, T, topo):
    rank = T.rank_of(core)
    if rank is None:
        return
    n_ranks = len(T.cores)
    V, S, P, Y = g.vector, g.scalar, g.tensor, g.sync
    eng = {"v": V, "s": S, "p": P, "y": Y, "g": g}
    ops = []

    def op(q, call, reads, writes, grp=None):
        ops.append((q, call, list(reads), list(writes), grp))

    def ts(out, in0, s1, s2, o0, o1, reads, writes):
        if o1 is None:
            op("v", lambda: V.tensor_scalar(out, in0, s1, None, o0), reads, writes)
        else:
            op("v", lambda: V.tensor_scalar(out, in0, s1, s2, o0, o1), reads, writes)

    def tt(out, in0, in1, o, reads, writes):
        op("v", lambda: V.tensor_tensor(out, in0, in1, o), reads, writes)

    def cp(out, in_, reads, writes):
        op("v", lambda: V.tensor_copy(out, in_), reads, writes)

    def ms(out, c, reads, writes):
        op("v", lambda: V.memset(out, c), reads, writes)

    def scan(out, d0, d1, init, o0, o1, reads, writes):
        op("v", lambda: V.tensor_tensor_scan(out, d0, d1, init, o0, o1), reads, writes)

    def mat(out, lhsT, rhs, start, stop, reads, writes, grp):
        op("p", lambda: P.matmul(out, lhsT, rhs, start, stop), reads, writes, grp)

    def iota(out, pattern, base, cm, key, flt=True):
        if flt:
            op("g", lambda: g.iota(out, pattern, base, cm, allow_small_or_imprecise_dtypes=True), [], [key])
        else:
            op("g", lambda: g.iota(out, pattern, base, cm), [], [key])

    def dma(out, in_, reads, writes):
        op("y", lambda: Y.dma_start(out, in_), reads, writes)

    ext = {}
    dests = []
    for t in range(RO):
        d = 1 + t % (n_ranks - 1)
        dst = T.cores[(rank + d) % n_ranks]
        src = T.cores[(rank - d) % n_ranks]
        dests.append(dst)
        got = len(topo.engines(src, core))
        ext[("rA", t)] = ("aA%d" % t, got)
        ext[("rB", t)] = ("aB%d" % t, got)
        if t == 0:
            ext["rR"] = ("aR", got)
    sent = [0]

    def remote(t, out, in_, sem, reads):
        dst = dests[t]
        rid, pid = topo.addr(dst)[0], topo.addr(dst)[1]
        mask = topo.mask(core, dst)
        sent[0] += len(topo.engines(core, dst))
        op("g", lambda: g.remote_dma(out, in_, T.sem[sem], T.sem.sent, pid, rid, mask), reads, [])

    dma(T.qS[:], T.q[:], [], ["q"])
    dma(T.tpS[:], T.tp[:], [], ["tp"])
    dma(T.domS[:, PAD:], T.dom[:], [], ["dom"])
    dma(T.valS[:, PAD:], T.val[:], [], ["val"])
    dma(T.ocS[:], T.oc[:], [], ["oc"])

    iota(T.pI[:, 0:1], [[0, 1]], 0, 1, "pI", False)
    iota(T.b16[:], [[16, 8], [0, 16]], 0, 0, "b16")
    iota(T.r16[:], [[0, 8], [1, 16]], 0, 0, "r16")
    iota(T.dif[:], [[1, 128]], 0, -1, "dif")
    iota(T.rowf[:], [[1, 144]], 0, 0, "rowf")
    ms(T.Z32[:], 0.0, [], ["Z320"])
    ts(T.cI[:, 0:1], T.pI[:, 0:1], 15, None, A.bitwise_and, None, ["pI"], ["cI0"])
    ts(T.cI[:, 1:2], T.pI[:, 0:1], 112, None, A.bitwise_and, None, ["pI"], ["cI1"])
    ts(T.cI[:, 2:3], T.pI[:, 0:1], 16, None, A.bitwise_and, None, ["pI"], ["cI2"])
    ms(T.Z32[:, 0:256:32], 2.0 * BIG, ["Z320"], ["Z32"])
    cp(T.cF[:, 0:3], T.cI[:, 0:3], ["cI0", "cI1", "cI2"], ["cF"])
    rcol, gcol, hcol = T.cF[:, 0:1], T.cF[:, 1:2], T.cF[:, 2:3]
    ms(T.Cb[:, 48:64], BIG, [], ["C3"])
    ts(T.t1[:], T.b16[:], gcol, 4096.0, A.is_equal, A.mult, ["b16", "cF"], ["t1"])
    ts(T.e1[:], T.r16[:, 0:16], rcol, None, A.is_equal, None, ["r16", "cF"], ["e1"])
    for r in list(range(1, 16)) + [0]:
        op("s", lambda r=r: S.activation(T.Lh[:, 128 * r:128 * r + 128], T.t1[:], F.Identity, scale=T.e1[:, r:r + 1]),
           ["t1", "e1"], [("L", r)])
    for r0 in (1, 6, 11):
        op("g", lambda r0=r0: g.affine_select(T.Wh[:, 128 * r0:128 * r0 + 640], T.Lh[:, 128 * r0:128 * r0 + 640],
                                              [[0, 5], [1, 128]], A.not_equal, -4096.0, 0, -1),
           [("L", r) for r in range(r0, r0 + 5)], [("W", r) for r in range(r0, r0 + 5)])
    ms(T.ZB[:], 0.0, [], ["ZB0"])
    ms(T.R01[:], 1.0, [], ["R0"])
    ms(T.ZB[:, 0:SL:16], 2.0 * BIG, ["ZB0"], ["ZB"])
    ms(T.R01[:, 0:SL:16], 0.0, ["R0"], ["R01"])
    ts(T.Ib[:], T.dif[:], 0.0, None, A.is_equal, None, ["dif"], ["Ib"])
    ts(T.mc[:, 0:1], hcol, 0.0, None, A.is_equal, None, ["cF"], ["mc0"])
    ts(T.mc[:, 1:2], hcol, 16.0, None, A.is_equal, None, ["cF"], ["mc1"])
    ts(T.e2[:], T.r16[:, 0:16], 1.0, rcol, A.add, A.is_equal, ["r16", "cF"], ["e2"])
    ts(T.t3[:], T.r16[:, 0:16], rcol, BIG, A.is_le, A.mult, ["r16", "cF"], ["t3"])
    ts(T.cF[:, 3:4], rcol, 16.0, None, A.add, None, ["cF"], ["cF3"])
    ts(T.tie[:], T.r16[:], -1.0 / 16, 15.0 / 16, A.mult, A.add, ["r16"], ["tie"])
    ts(T.Zl[:], T.rowf[:], gcol, 15.0, A.subtract, A.is_equal, ["rowf", "cF"], ["Zl"])
    ts(T.Cb[:, 0:16], T.t3[:], rcol, None, A.max, None, ["t3", "cF"], ["C0"])
    ts(T.Cb[:, 16:32], T.t3[:], 0.0, rcol, A.mult, A.add, ["t3", "cF"], ["C1"])
    ts(T.Cb[:, 32:48], T.t3[:], T.cF[:, 3:4], None, A.max, None, ["t3", "cF3"], ["C2"])
    tt(T.Dm[:], T.e1[:], T.e2[:], A.subtract, ["e1", "e2"], ["Dm"])
    cp(T.Cb[:, 64:128], T.Cb[:, 0:64], ["C0", "C1", "C2", "C3"], ["C4"])
    cp(T.ou[:, 0:8], T.qS[:], ["q"], ["uraw"])
    cp(T.Cb[:, 128:256], T.Cb[:, 0:128], ["C0", "C1", "C2", "C3", "C4"], ["C5"])
    ts(T.sB[:, 15:128:16], T.qS[:], -1024.0, None, A.add, None, ["q"], ["sB"])
    ms(T.Cb[:, 0:256:32], 1024.0 + PAD, [], ["C0", "C2", "C4", "C5", "Cb"])
    ts(T.nI4[:], T.dif[:], 0.0, -4096.0, A.is_equal, A.mult, ["dif"], ["nI4"])
    ms(T.xA[:, NV:NV + PAD], 0.0, [], ["xpad"])
    cp(T.lane[:], T.rowf[:, 0:128], ["rowf"], ["lane"])

    def twins(h, s, skey, parts=(0, 1)):
        if 0 in parts:
            mat(T.pD[:, 0:256], T.Ib[:], T.Cb[:], True, False, ["Ib", "Cb"], ["pD"], ("D", h))
            for r in range(16):
                mat(T.pD[:, 16 + r:256:64], T.nI4[:], s[:, 15:128:32], False, False, ["nI4", skey], ["pD"], ("D", h))
            for r in range(16):
                mat(T.pD[:, 16 + r:256:64], T.Lh[:, 128 * r:128 * r + 128], s[:, 31:128:32], False, False,
                    [("L", r), skey], ["pD"], ("D", h))
        if 1 in parts:
            for r in range(16):
                mat(T.pD[:, r:256:32], T.Wh[:, 128 * r:128 * r + 128] if r else T.Ib[:], s[:, 15:128:16], False, r == 15,
                    [("W", r), skey], ["pD"], ("D", h))

    def absd():
        op("s", lambda: S.activation(T.yy[:], T.pD[:, 0:256], F.Abs), ["pD"], ["yy"])

    def ddscan():
        scan(T.dd[:], T.Z32[:], T.yy[:], 0.0, A.add, A.min, ["Z32", "yy"], ["dd"])

    def ddlist(buf, key):
        cp(buf[:, 8:OW], T.dd[:, 31:256:32], ["dd"], [key])

    def pointers(p, pkey, tab, tkey, lst, lkey):
        cp(p[:], tab[:].indirect(lst), [tkey, lkey], [pkey])

    def halves(p, pkey, e):
        ts(T.pm[:, 128 * e:128 * e + 128], p[:], -1024.0, T.mc[:, e:e + 1], A.add, A.mult, [pkey, "mc%d" % e], [("pm", e)])

    def turn(h):
        for a in range(4):
            for c in range(8):
                mat(T.pP[32 * a:32 * a + 32, 16 * c:16 * c + 16], T.pm[32 * a:32 * a + 32, c:256:8],
                    T.Dm[32 * a:32 * a + 32, :], True, True, [("pm", 0), ("pm", 1), "Dm"], ["pP"], ("P", h))

    def kfirst(h):
        mat(T.pK[:, 0:128], T.Ib[:], T.tie[:], True, False, ["Ib", "tie"], ["pK"], ("K", h))

    def ksums(h, x, xn, k0, k1):
        for k in range(k0, k1):
            mat(T.pK[:, 0:128], T.Zl[:, 15 - k:143 - k], x[:, 128 * k:128 * k + 128], False, k == 15,
                ["Zl", (xn, k)], ["pK"], ("K", h))

    def total(ps, key, tab, tkey, n, out, okey):
        for k in range(n // 128):
            mat(ps[:, 0:128], T.Ib[:], tab[:, PAD + 128 * k:PAD + 128 * k + 128], k == 0, k == n // 128 - 1,
                ["Ib", tkey], [key], key)
        op("s", lambda: S.activation(T.junk[:], ps[:, 0:128], F.Identity, accum_out=out), [key], ["junk", okey])

    def gather(q, x, xn, tab, tkey, p, pkey, k0, k1):
        src = tab[:, PAD:].indirect(p[:, 8 * k0:8 * k1])
        out = x[:, 128 * k0:128 * k1]
        keys = [(xn, k) for k in range(k0, k1)]
        if q == "v":
            cp(out, src, [tkey, pkey], keys)
        else:
            op("s", lambda: S.activation(out, src, F.Copy), [tkey, pkey], keys)

    def fold(w, wn, x, xn, k0, k1, low):
        n = 128 * (k1 - k0)
        reads = [(xn, k) for k in range(k0, k1)]
        keys = [(wn, k) for k in range(k0, k1)]
        if low:
            scan(w[:, 128 * k0:128 * k1], T.ZB[:, 0:n], x[:, 128 * k0:128 * k1], 0.0, A.add, A.min, reads + ["ZB"], keys)
        else:
            scan(w[:, 128 * k0:128 * k1], T.R01[:, 0:n], x[:, 128 * k0:128 * k1], 0.0, A.mult, A.max, reads + ["R01"], keys)

    def best1():
        scan(T.mx[:], T.R01[:, 0:128], T.pK[:, 0:128], 0.0, A.mult, A.max, ["R01", "pK"], ["mx"])

    def best2():
        tt(T.ne[:], T.pK[:, 0:128], T.mx[:], A.is_lt, ["pK", "mx"], ["ne"])

    def best3(s, skey):
        scan(s[:], T.ne[:], T.pP[:, 0:128], 0.0, A.mult, A.add, ["ne", "pP"], [skey])

    def best4(out, s, skey, key):
        ts(out, s[:, 15:128:16], 1024.0, None, A.add, None, [skey], [key])

    def scat(tab, tkeys, lst, lkey, c, src, skeys):
        cp(tab[:].indirect(lst[:, 8 + 2 * c:10 + 2 * c]), src, [lkey] + skeys, tkeys)

    kfirst("0a")
    twins("0a", T.sB, "sB", (0,))
    pointers(T.pA, "pA", T.tpS, "tp", T.ou[:, 0:8], "uraw")
    halves(T.pA, "pA", 0)
    halves(T.pA, "pA", 1)
    turn("0a")

    for t in range(RO):
        ha, hb = "%da" % t, "%db" % t
        first, last = t == 0, t == RO - 1
        mt = T.mm[:, NL * t:NL * t + NL]
        rmt = T.rm[:, NL * t:NL * t + NL]
        rk = ("rA", t)

        def lst(buf, c0, c1):
            return buf[:, OW * t + c0:OW * t + c1]

        def put(tab, tkeys, buf, lkey, c, src, skeys):
            cp(tab[:].indirect(lst(buf, 8 + 2 * c, 10 + 2 * c)), src, [lkey] + skeys, tkeys)

        def wsc(c):
            scat(T.valS, ["val"], T.ou, "udd", c, T.wsA[:, 512 * c + 15:512 * c + 512:16],
                 [("wA", k) for k in range(4 * c, 4 * c + 4)])

        def msc(c):
            put(T.domS, ["dom"], T.oa, ("add", t), c, T.mm[:, NL * t + 32 * c:NL * t + 32 * c + 32], [("m", t)])

        nv, (e1, e2, e3) = PLAN1
        gather("v", T.xA, "xA", T.domS, "dom", T.pA, "pA", 0, nv)
        gather("s", T.xA, "xA", T.domS, "dom", T.pA, "pA", nv, e1)
        gather("s", T.xA, "xA", T.domS, "dom", T.pA, "pA", e1, e2)
        gather("s", T.xA, "xA", T.domS, "dom", T.pA, "pA", e2, e3)
        if first:
            ksums(ha, T.xA, "xA", 0, nv)
            twins(ha, T.sB, "sB", (1,))
            ksums(ha, T.xA, "xA", nv, 16)
            absd()
            fold(T.wsA, "wA", T.xA, "xA", 0, nv, True)
            fold(T.wsA, "wA", T.xA, "xA", nv, e1, True)
            fold(T.wsA, "wA", T.xA, "xA", e1, e2, True)
            best1()
            ddscan()
            best2()
            ddlist(T.ou, "udd")
            best3(T.sA, "sA")
            wsc(0)
            best4(lst(T.oa, 0, 8), T.sA, "sA", ("araw", t))
            remote(t, lst(T.ro, 0, 8), lst(T.oa, 0, 8), "aR", [("araw", t), "oc"])
            wsc(1)
            fold(T.wsA, "wA", T.xA, "xA", e2, e3, True)
            wsc(2)
            wsc(3)
            pointers(T.pB, "pB", T.ocS, "oc", lst(T.oa, 0, 8), ("araw", t))
        else:
            ksums(ha, T.xA, "xA", 0, 16)
            ddscan()
            fold(T.wsA, "wA", T.xA, "xA", 0, nv, True)
            ddlist(T.ou, "udd")
            fold(T.wsA, "wA", T.xA, "xA", nv, e1, True)
            wsc(0)
            fold(T.wsA, "wA", T.xA, "xA", e1, e2, True)
            best1()
            fold(T.wsA, "wA", T.xA, "xA", e2, e3, True)
            best2()
            wsc(1)
            best3(T.sA, "sA")
            wsc(2)
            best4(lst(T.oa, 0, 8), T.sA, "sA", ("araw", t))
            wsc(3)
            pointers(T.pB, "pB", T.ocS, "oc", lst(T.oa, 0, 8), ("araw", t))

        nv, (e1, e2, e3) = PLAN2
        twins(hb, T.sA, "sA")
        kfirst(hb)
        gather("v", T.xB, "xB", T.valS, "val", T.pB, "pB", 0, nv)
        gather("s", T.xB, "xB", T.valS, "val", T.pB, "pB", nv, e1)
        absd()
        gather("s", T.xB, "xB", T.valS, "val", T.pB, "pB", e1, e2)
        gather("s", T.xB, "xB", T.valS, "val", T.pB, "pB", e2, e3)
        ksums(hb, T.xB, "xB", 0, 16)
        halves(T.pB, "pB", 0)
        fold(T.wsB, "wB", T.xB, "xB", 0, nv, False)
        fold(T.wsB, "wB", T.xB, "xB", nv, e1, False)
        ddscan()
        halves(T.pB, "pB", 1)
        turn(hb)
        ddlist(T.oa[:, OW * t:OW * t + OW], ("add", t))
        c0 = 8 if first else 0
        remote(t, lst(T.ro, c0, OW), lst(T.oa, c0, OW), "aA%d" % t, [("araw", t), ("add", t)])
        fold(T.wsB, "wB", T.xB, "xB", e1, e2, False)
        fold(T.wsB, "wB", T.xB, "xB", e2, e3, False)
        tt(mt, T.domS[:, PAD:].indirect(lst(T.oa, 0, 8)), T.wsB[:, 15:NV:16], A.min,
           ["dom", ("araw", t)] + [("wB", k) for k in range(16)], [("m", t)])
        remote(t, rmt, mt, "aB%d" % t, [("m", t)])

        if not last:
            hn = "%da" % (t + 1)
            best1()
            msc(0)
            best2()
            msc(1)
            best3(T.sB, "sB")
            msc(2)
            best4(T.ou[:, 0:8], T.sB, "sB", "uraw")
            kfirst(hn)
            twins(hn, T.sB, "sB")
            absd()
            msc(3)
            pointers(T.pA, "pA", T.tpS, "tp", T.ou[:, 0:8], "uraw")

            def rsc(c):
                put(T.domS, ["dom"], T.ro, rk, c, T.nw[:, 32 * c:32 * c + 32], ["nw"])

            tt(T.nw[:], T.domS[:, PAD:].indirect(lst(T.ro, 0, 8)), rmt, A.min,
               ["dom", rk, ("rB", t)] + (["rR"] if first else []), ["nw"])
            rsc(0)
            halves(T.pA, "pA", 0)
            rsc(1)
            halves(T.pA, "pA", 1)
            rsc(2)
            rsc(3)
            turn(hn)
        else:
            tag = [("xA", k) for k in range(16)] + ["xpad"]

            def mark(c):
                put(T.xA, tag, T.ro, rk, c, T.lane[:, 32 * c:32 * c + 32], ["lane"])

            dma(T.yv[:], mt, [("m", t)], ["yv"])
            op("s", lambda: S.activation(T.wide[:], T.valS[:, PAD:], F.Identity, accum_out=T.fin[:, 128:129]),
               ["val"], ["sumv"])
            best1()
            msc(0)
            best2()
            msc(1)
            mark(0)
            msc(2)
            mark(1)
            msc(3)
            total(T.pSD, "pSD", T.domS, "dom", NV, T.basec[:, 0:1], "base")
            mark(2)
            best3(T.sB, "sB")
            mark(3)
            best4(T.ytS[:], T.sB, "sB", "ytS")
            dma(T.yt[:], T.ytS[:], ["ytS"], ["yt"])
            tt(T.win[:], T.xA[:, PAD:].indirect(lst(T.ro, 0, 8)), T.lane[:], A.is_equal, tag + ["lane", rk], ["win"])
            tt(T.nw[:], T.domS[:, PAD:].indirect(lst(T.ro, 0, 8)), T.win[:], A.mult, ["dom", "win", rk], ["nw"])
            tt(T.win[:], T.nw[:], rmt, A.min, ["nw", ("rB", t)], ["win"])
            scan(T.fin[:, 0:128], T.win[:], T.nw[:], T.basec[:, 0:1], A.add, A.subtract, ["win", "nw", "base"], ["fin"])
            dma(T.ys[:], T.fin[:, 127:129], ["fin", "sumv"], ["ys"])

    op("y", None, ["yv", "yt", "ys"], [])
    schedule(ops, ext, eng, T)
    g.wait_ge(T.sem.sent, sent[0])
